import numpy as np
import ml_dtypes


def mxq(x, axis, fmt="e4m3"):
    dtype, down = {"e4m3": (ml_dtypes.float8_e4m3fn, 7), "e5m2": (ml_dtypes.float8_e5m2, 14)}[fmt]
    v = np.moveaxis(np.asarray(x, np.float32).astype(ml_dtypes.bfloat16).astype(np.float64), axis, -1)
    blocks = v.reshape(v.shape[:-1] + (-1, 32))
    amax = np.abs(blocks).max(-1, keepdims=True)
    byte = np.maximum(np.where(amax > 0, np.frexp(amax)[1] - 1 + 127, 0) - down, 1)
    scale = np.exp2(byte - 127.0)
    codes = (blocks / scale).astype(np.float32).astype(dtype).astype(np.float64)
    return np.moveaxis((codes * scale).reshape(v.shape), -1, axis)


WIDE = False


def mx_kscale(k):
    if not WIDE:
        return np.ones(k)
    levels = np.array([10, -10, 5, -5, 0])
    if k % 512:
        return np.exp2(np.random.permutation(np.resize(levels, k // 32))).repeat(32)
    a = np.empty((k // 512, 16))
    for p in range(k // 512):
        a[p, :8] = np.random.permutation(np.resize(levels, 8))
        for g in range(8):
            far = levels[np.abs(levels - a[p, g]) >= 10]
            a[p, g + 8] = far[np.random.randint(len(far))]
    return np.exp2(a.ravel()).repeat(32)


def f64(x):
    return np.asarray(x).astype(np.float64)


def striped(idx):
    return np.tile(idx.reshape(-1, 16).T, (8, 1)).astype(np.uint16)


def unstriped(offs):
    return offs[:16].T.reshape(-1).astype(np.int64)


E2M1 = np.array([0.0, 0.5, 1.0, 1.5, 2.0, 3.0, 4.0, 6.0, -0.0, -0.5, -1.0, -1.5, -2.0, -3.0, -4.0, -6.0])


def pack_weight(w, fmt):
    k, n = w.shape
    w = f64(np.asarray(w, np.float32).astype(ml_dtypes.bfloat16)).reshape(k // 32, 32, n)
    amax = np.abs(w).max(1)
    if fmt == "e4m3":
        byte = np.frexp(amax)[1] - 1 + 127 - 7
    else:
        mant, ex = np.frexp(amax / 6.0)
        byte = np.where(mant > 0.5, ex, ex - 1) + 127
    byte = np.clip(np.where(amax > 0, byte, 1), 1, 254)
    scaled = (w * np.exp2(127.0 - byte)[:, None, :]).reshape(k, n).astype(np.float32)
    by_word = np.ascontiguousarray(scaled.reshape(k // 512, 128, 4, n).transpose(0, 1, 3, 2))
    if fmt == "e4m3":
        words = by_word.astype(ml_dtypes.float8_e4m3fn).view(np.uint8)
    else:
        c = by_word.astype(ml_dtypes.float4_e2m1fn).view(np.uint8) & 0xF
        words = (c[..., 0::2] | (c[..., 1::2] << 4)).reshape(k // 512, 128, 2 * n)
    return np.ascontiguousarray(words), np.ascontiguousarray(byte.astype(np.uint8).reshape(k // 512, 16, n))


def unpack_weight(words, scales, fmt):
    g, _, n = scales.shape
    words = np.ascontiguousarray(words).reshape(g, 128, n, -1)
    if fmt == "e4m3":
        vals = words.view(ml_dtypes.float8_e4m3fn).astype(np.float64)
    else:
        nib = np.empty((g, 128, n, 4), np.uint8)
        nib[..., 0::2] = words & 0xF
        nib[..., 1::2] = words >> 4
        vals = E2M1[nib]
    vals = vals * np.repeat(np.exp2(scales.astype(np.float64) - 127.0), 8, axis=1)[..., None]
    return vals.transpose(0, 1, 3, 2).reshape(g * 512, n)


def gelu(v):
    return 0.5 * v * (1.0 + np.tanh(np.sqrt(2.0 / np.pi) * (v + 0.044715 * v**3)))


K, KA, KB, T, H, S, S2, T3, P = 1536, 512, 1024, 4096, 1024, 1024, 512, 2048, 512

def setup_inputs():
    n = np.random.standard_normal
    s = mx_kscale(K)[:, None]
    u = mx_kscale(H)[:, None]
    tab_words, tab_scales = pack_weight(n((K, T)) * s, "e4m3")
    tab2_words, tab2_scales = pack_weight(n((H, T3)) / np.sqrt(H) / u, "e4m3")
    w4_words, w4_scales = pack_weight(n((KB, H)) / np.sqrt(K) / s[KA:], "e2m1")
    return {
        "tab_words": tab_words, "tab_scales": tab_scales,
        "offs": striped(np.random.permutation(T)[:S]),
        "w1": (n((KA, H)) / np.sqrt(K) / s[:KA]).astype(np.float32),
        "w4_words": w4_words, "w4_scales": w4_scales,
        "shelf": n((H, S)).astype(np.float32),
        "gain": (np.exp(0.3 * n(H)) * u[:, 0]).astype(np.float32),
        "pos1": striped(np.random.permutation(S)[:P]),
        "pos2": striped(np.random.permutation(S)[:P]),
        "cap": (0.4 * n(H) * u[:, 0]).astype(np.float32),
        "tab2_words": tab2_words, "tab2_scales": tab2_scales,
        "offs2": striped(np.random.permutation(T3)[:S2]),
        "fit": np.exp(0.3 * n((S2, P))).astype(np.float32),
    }

def reference(tab_words, tab_scales, offs, w1, w4_words, w4_scales, shelf, gain, pos1, pos2, cap, tab2_words, tab2_scales, offs2, fit):
    v = unpack_weight(tab_words, tab_scales, "e4m3")[:, unstriped(offs)]
    v2 = unpack_weight(tab2_words, tab2_scales, "e4m3")[:, unstriped(offs2)]
    w1q = mxq(f64(w1), 0, "e4m3")
    w4 = unpack_weight(w4_words, w4_scales, "e2m1")
    a = w1q.T @ v[:KA] + w4.T @ v[KA:]
    h = f64(gain)[:, None] * np.tanh(a + f64(shelf))
    x1 = mxq(np.minimum(h[:, unstriped(pos1)], f64(cap)[:, None]), 0, "e4m3")
    x2 = mxq(np.abs(h[:, unstriped(pos2)]), 0, "e4m3")
    e = v2.T @ x1 + v2.T @ x2
    return f64(fit) * e

@@ -1,0 +1,274 @@
+from contextlib import ExitStack
+
+import concourse.mybir as mybir
+
+K, T, H, S, S2, T3, NP = 1536, 4096, 1024, 1024, 512, 2048, 512
+FLOPS = 2 * K * H * S + 2 * 2 * H * S2 * NP
+
+F32 = mybir.dt.float32
+BF16 = mybir.dt.bfloat16
+I32 = mybir.dt.int32
+U32 = mybir.dt.uint32
+U16 = mybir.dt.uint16
+U8 = mybir.dt.uint8
+FP8X4 = mybir.dt.float8_e4m3fn_x4
+FP4X4 = mybir.dt.float4_e2m1fn_x4
+ALU = mybir.AluOpType
+ACT = mybir.ActivationFunctionType
+
+P = 128
+HALF = 512
+PAIRS = 256
+CLEAR = 5632
+
+
+def tile_list_shelf_neighbour_features_kernel(
+    tc, tab_words, tab_scales, offs, w1, w4_words, w4_scales, shelf, gain, pos1, pos2, cap,
+    tab2_words, tab2_scales, offs2, fit, out,
+):
+    nc = tc.nc
+    with ExitStack() as ctx:
+        keep = ctx.enter_context(tc.tile_pool(name="keep", bufs=1))
+        big = ctx.enter_context(tc.tile_pool(name="big", bufs=3))
+        work = ctx.enter_context(tc.tile_pool(name="work", bufs=2))
+        psum = ctx.enter_context(tc.psum_pool(name="psum", bufs=4))
+
+        def load_list(src, name):
+            tile = keep.tile([P, src.shape[1]], U16, name=name)
+            nc.sync.dma_start(tile[:], src)
+            return tile
+
+        def kept(shape, dtype, name):
+            return keep.tile(shape, dtype, name=name, align_bytes=64)
+
+        w4s_raw = kept([P, 2, H], U8, "w4s_raw")
+        nc.gpsimd.memset(w4s_raw[:].rearrange("p a c -> p (a c)").bitcast(I32), 0)
+        tabs = keep.tile([P, 2 * T], U8, name="tabs", tag="tabs", align_bytes=64)
+        nc.vector.memset(tabs[:, :CLEAR].bitcast(I32), 0)
+        nc.gpsimd.memset(tabs[:, CLEAR:].bitcast(I32), 0)
+        tab2s = kept([P, T3], U8, "tab2s")
+        nc.gpsimd.memset(tab2s[:].bitcast(I32), 0)
+
+        idx = load_list(offs, "idx")
+        w4_raw = kept([P, 2, 2 * H], U8, "w4_raw")
+        nc.sync.dma_start(w4_raw[:].bitcast(I32), w4_words.rearrange("a p c -> p a c").bitcast(I32))
+
+        for r in range(4):
+            nc.sync.dma_start(w4s_raw[r:P:32, :, :].bitcast(I32),
+                                w4_scales[:, r:16:4, :].rearrange("a q c -> q a c").bitcast(I32))
+
+        def load_table(a):
+            tile = big.tile([P, T], I32, name=f"tab{a}", tag="big", align_bytes=64)
+            nc.sync.dma_start(tile[:], tab_words[a].rearrange("p t i -> p (t i)").bitcast(I32))
+            return tile
+
+        def load_w1(b, tile):
+            nc.sync.dma_start(tile[:], w1[:, b * HALF:(b + 1) * HALF].rearrange("(p i) c -> p i c", i=4))
+
+        tab = {1: load_table(1)}
+        for r in range(4):
+            nc.sync.dma_start(tabs[r:P:32, :].bitcast(I32).rearrange("q (a c) -> q a c", a=2),
+                              tab_scales[1:3, r:16:4, :].rearrange("a q c -> q a c").bitcast(I32))
+        tab[2] = load_table(2)
+        for q in (0, 2, 1, 3):
+            nc.sync.dma_start(tabs[32 * q + 4:32 * q + 8, T:].bitcast(I32), tab_scales[0, 4 * q:4 * q + 4, :].bitcast(I32))
+        w1_raw = [kept([P, 4, HALF], F32, "w1_raw0")]
+        load_w1(0, w1_raw[0])
+        idx2 = load_list(offs2, "idx2")
+        for q in range(4):
+            nc.sync.dma_start(tab2s[32 * q:32 * q + 8, :].bitcast(I32),
+                              tab2_scales[:, 4 * q:4 * q + 4, :].bitcast(I32))
+        tab[0] = load_table(0)
+        left = load_list(pos1, "left")
+        right = load_list(pos2, "right")
+        gain_sb = kept([P, 2, 4], F32, "gain_sb")
+        nc.sync.dma_start(gain_sb[:], gain.rearrange("(b p t) -> p b t", b=2, t=4))
+        cap_sb = kept([P, 2, 4], F32, "cap_sb")
+        nc.sync.dma_start(cap_sb[:], cap.rearrange("(b p t) -> p b t", b=2, t=4))
+
+        shelf_rows = shelf.rearrange("(b p t) j -> b t p j", b=2, t=4)
+        pre = {}
+
+        def load_shelf(b):
+            for t in range(4):
+                pre[b, t] = kept([P, S], F32, f"pre{b}{t}")
+                nc.sync.dma_start(pre[b, t][:], shelf_rows[b, t])
+
+        load_shelf(0)
+        w1_raw.append(big.tile([P, 4, HALF], F32, name="w1_raw1", tag="big", align_bytes=64))
+        load_w1(1, w1_raw[1])
+        tab2 = big.tile([P, 2, T3], I32, name="tab2", tag="big", align_bytes=64)
+        nc.sync.dma_start(tab2[:], tab2_words.rearrange("a p t i -> p a (t i)").bitcast(I32))
+        load_shelf(1)
+        fit_sb = big.tile([P, 4, NP], F32, name="fit_sb", tag="big", align_bytes=64)
+        nc.sync.dma_start(fit_sb[:], fit.rearrange("(m p) j -> p m j", p=P))
+
+        w4_dealt = kept([P, 4, 4, 2 * P], U8, "w4_dealt")
+        nc.vector.tensor_copy(w4_dealt[:].bitcast(U16),
+                              w4_raw[:].bitcast(U16).rearrange("p a (b m t) -> p (a b) t m", b=2, t=4))
+        w4s_dealt = kept([P, 4, 4, P], U8, "w4s_dealt")
+        nc.vector.tensor_copy(w4s_dealt[:], w4s_raw[:].rearrange("p a (b m t) -> p (a b) t m", b=2, t=4))
+
+        w1_bf, w1_codes, w1_scales = {}, {}, {}
+
+        def round_w1(b):
+            w1_bf[b] = work.tile([P, 4 * HALF], BF16, name="w1_bf", tag="woven", bufs=3, align_bytes=64)
+            nc.scalar.copy(w1_bf[b][:].rearrange("p (t m i) -> p m t i", t=4, i=4),
+                           w1_raw[b][:].rearrange("p i (m t) -> p m t i", t=4))
+
+        def quantize_w1(b):
+            w1_codes[b] = kept([P, HALF], U32, f"w1_codes{b}")
+            w1_scales[b] = kept([P, HALF], U8, f"w1_scales{b}")
+            nc.vector.quantize_mx(out=w1_codes[b][:].bitcast(FP8X4), scales=w1_scales[b][:], in_=w1_bf[b][:])
+
+        v_words = {a: kept([P, S], U32, f"v_words{a}") for a in (1, 2)}
+        v_scales = [kept([P, S], U8, f"v_scales{w}") for w in range(2)]
+
+        def first_stage_pass(acc, a, b, t, h, start, stop):
+            cols = slice(h * HALF, (h + 1) * HALF)
+            if a == 0:
+                ch = slice(t * P, (t + 1) * P)
+                lhsT, lhsT_scale = w1_codes[b][:, ch].bitcast(FP8X4), w1_scales[b][:, ch]
+                rhs_scale = v_scales[1][4:P, cols]
+            else:
+                lhsT, lhsT_scale = w4_dealt[:, 2 * (a - 1) + b, t, :].bitcast(FP4X4), w4s_dealt[:, 2 * (a - 1) + b, t, :]
+                rhs_scale = v_scales[a - 1][:, cols]
+            nc.tensor.matmul_mx(out=acc[:], lhsT=lhsT, lhsT_scale=lhsT_scale,
+                                rhs=v_words[a][:, cols].bitcast(FP8X4), rhs_scale=rhs_scale,
+                                start=start, stop=stop)
+
+        nc.vector.tensor_copy(v_words[1][:], tab[1][:].bitcast(U32).indirect(idx[:]))
+        nc.vector.tensor_copy(v_scales[0][:], tabs[:, :T].indirect(idx[:]))
+        nc.vector.tensor_copy(v_words[2][:], tab[2][:].bitcast(U32).indirect(idx[:]))
+        nc.vector.tensor_copy(v_scales[1][:], tabs[:, T:].indirect(idx[:]))
+        round_w1(0)
+        v2_scales = kept([P, S2], U8, "v2_scales")
+        nc.vector.tensor_copy(v2_scales[:], tab2s[:].indirect(idx2[:]))
+        quantize_w1(0)
+
+        v_words[0] = keep.tile([P, S], U32, name="v_words0", tag="tabs", align_bytes=64)
+        acc = {}
+        for t in range(4):
+            for h in range(2):
+                acc[0, t, h] = psum.tile([P, HALF], F32, name="acc", tag="early" if t < 2 else "late")
+        for a in (1, 2):
+            for t in range(4):
+                for h in range(2):
+                    first_stage_pass(acc[0, t, h], a, 0, t, h, a == 1, False)
+        for h in range(2):
+            nc.vector.tensor_copy(v_words[0][:, h * HALF:(h + 1) * HALF],
+                                  tab[0][:].bitcast(U32).indirect(idx[:, h * 32:(h + 1) * 32]))
+            for t in range(4):
+                first_stage_pass(acc[0, t, h], 0, 0, t, h, False, True)
+
+        hidden = {}
+
+        def make_hidden(b, t):
+            for h in range(2):
+                if b == 1:
+                    acc[b, t, h] = psum.tile([P, HALF], F32, name="acc", tag="early")
+                    for a in (1, 2, 0):
+                        first_stage_pass(acc[b, t, h], a, b, t, h, a == 1, a == 0)
+                cols = slice(h * HALF, (h + 1) * HALF)
+                nc.vector.tensor_tensor(pre[b, t][:, cols], acc[b, t, h][:], pre[b, t][:, cols], ALU.add)
+            nc.scalar.activation(pre[b, t][:], pre[b, t][:], ACT.Tanh)
+            hidden[b, t] = work.tile([P, S], F32, name="hidden", bufs=5)
+            nc.scalar.activation(hidden[b, t][:], pre[b, t][:], ACT.Copy, scale=gain_sb[:, b, t:t + 1])
+
+        def picked_tile(shape, tag):
+            return work.tile(shape, F32, name="picked", tag=tag, bufs=1, align_bytes=64)
+
+        def pick(dst, b, t, offsets):
+            nc.vector.tensor_copy(dst[:, t, :], hidden[b, t][:].indirect(offsets))
+
+        def cap_plane(dst, src, b, t):
+            nc.vector.tensor_scalar(dst[:, t, :], src[:, t, :], cap_sb[:, b, t:t + 1], None, ALU.min)
+
+        def woven_tile(width):
+            return work.tile([P, width, 4], BF16, name="woven", tag="woven", bufs=3, align_bytes=64)
+
+        def weave(planes):
+            woven = woven_tile(planes.shape[2])
+            nc.scalar.copy(woven[:], planes.rearrange("p t j -> p j t"))
+            return woven
+
+        def weave_abs(planes):
+            woven = woven_tile(planes.shape[2])
+            nc.scalar.activation(woven[:], planes.rearrange("p t j -> p j t"), ACT.Abs)
+            return woven
+
+        def quantize(woven):
+            width = woven.shape[1]
+            codes = work.tile([P, width], U32, name="codes", bufs=3, align_bytes=64)
+            scales = work.tile([P, width], U8, name="scales", bufs=3, align_bytes=64)
+            nc.vector.quantize_mx(out=codes[:].bitcast(FP8X4), scales=scales[:],
+                                  in_=woven[:].rearrange("p j t -> p (j t)"))
+            return codes, scales
+
+        v2_words = kept([P, 2, S2], U32, "v2_words")
+        sums = {}
+
+        def second_stage(operand, b, halves, start, stop):
+            codes, scales = operand
+            for n, half in enumerate(halves):
+                cols = slice(n * PAIRS, (n + 1) * PAIRS)
+                for g in range(2):
+                    if start:
+                        sums[g, half] = psum.tile([P, 2, PAIRS], F32, name="sums", tag="late")
+                    for u in range(2):
+                        m = slice((2 * g + u) * P, (2 * g + u + 1) * P)
+                        nc.tensor.matmul_mx(out=sums[g, half][:, u, :],
+                                            lhsT=v2_words[:, b, m].bitcast(FP8X4), lhsT_scale=v2_scales[4 * b:P, m],
+                                            rhs=codes[:, cols].bitcast(FP8X4), rhs_scale=scales[:, cols],
+                                            start=start and u == 0, stop=stop and u == 1)
+
+        out_rows = out.rearrange("(m p) j -> p m j", p=P)
+
+        def finish(half):
+            cols = slice(half * PAIRS, (half + 1) * PAIRS)
+            for g in range(2):
+                result = work.tile([P, 2, PAIRS], F32, name="result", bufs=4)
+                nc.vector.tensor_tensor(result[:], sums[g, half][:], fit_sb[:, 2 * g:2 * g + 2, cols], ALU.mult)
+                nc.sync.dma_start(out_rows[:, 2 * g:2 * g + 2, cols], result[:])
+
+        for t in range(3):
+            make_hidden(0, t)
+        round_w1(1)
+        lefts, rights = picked_tile([P, 4, NP], "picked_a"), picked_tile([P, 4, NP], "picked_b")
+        capped = work.tile([P, 4, NP], BF16, name="capped")
+        ahead = [(0, 3), None, (1, 0), (1, 1)]
+        for t in range(4):
+            pick(lefts, 0, t, left[:])
+            pick(rights, 0, t, right[:])
+            cap_plane(capped, lefts, 0, t)
+            if ahead[t] is None:
+                quantize_w1(1)
+            else:
+                make_hidden(*ahead[t])
+        x1_woven, x2_woven = weave(capped[:]), weave_abs(rights[:])
+        for a in range(2):
+            nc.vector.tensor_copy(v2_words[:, a, :], tab2[:, a, :].bitcast(U32).indirect(idx2[:]))
+
+        lefts = picked_tile([P, 4, NP], "picked_a")
+        capped = work.tile([P, 4, NP], BF16, name="capped")
+        for t in range(4):
+            pick(lefts, 1, t, left[:])
+            if t < 2:
+                make_hidden(1, t + 2)
+            elif t == 2:
+                second_stage(quantize(x1_woven), 0, (0, 1), True, False)
+            else:
+                second_stage(quantize(x2_woven), 0, (0, 1), False, False)
+            cap_plane(capped, lefts, 1, t)
+        x1_woven = weave(capped[:])
+        rights = picked_tile([P, 2, 4, PAIRS], "picked_a")
+        halves = []
+        for half in range(2):
+            for t in range(4):
+                pick(rights[:, half, :, :], 1, t, right[:, half * 16:(half + 1) * 16])
+            halves.append(weave_abs(rights[:, half, :, :]))
+            if half == 0:
+                second_stage(quantize(x1_woven), 1, (0, 1), False, False)
+        for half in range(2):
+            second_stage(quantize(halves[half]), 1, (half,), False, True)
+            finish(half)

@@ -46,8 +46,8 @@ def tile_list_shelf_neighbour_features_kernel(
         tabs = keep.tile([P, 2 * T], U8, name="tabs", tag="tabs", align_bytes=64)
         nc.vector.memset(tabs[:, :CLEAR].bitcast(I32), 0)
         nc.gpsimd.memset(tabs[:, CLEAR:].bitcast(I32), 0)
-        tab2s = kept([P, T3], U8, "tab2s")
-        nc.gpsimd.memset(tab2s[:].bitcast(I32), 0)
+        tab2s = keep.tile([P, T3], U8, name="tab2s", tag="tab2s", align_bytes=64)
+        nc.vector.memset(tab2s[:].bitcast(I32), 0)
 
         idx = load_list(offs, "idx")
         w4_raw = kept([P, 2, 2 * H], U8, "w4_raw")
@@ -67,17 +67,16 @@ def tile_list_shelf_neighbour_features_kernel(
 
         tab = {1: load_table(1)}
         for r in range(4):
-            nc.sync.dma_start(tabs[r:P:32, :].bitcast(I32).rearrange("q (a c) -> q a c", a=2),
-                              tab_scales[1:3, r:16:4, :].rearrange("a q c -> q a c").bitcast(I32))
+            nc.gpsimd.dma_start(tabs[r:P:32, :].bitcast(I32).rearrange("q (a c) -> q a c", a=2),
+                                tab_scales[1:3, r:16:4, :].rearrange("a q c -> q a c").bitcast(I32))
+            nc.gpsimd.dma_start(tabs[4 + r:P:32, T:].bitcast(I32), tab_scales[0, r:16:4, :].bitcast(I32))
         tab[2] = load_table(2)
-        for q in (0, 2, 1, 3):
-            nc.sync.dma_start(tabs[32 * q + 4:32 * q + 8, T:].bitcast(I32), tab_scales[0, 4 * q:4 * q + 4, :].bitcast(I32))
         w1_raw = [kept([P, 4, HALF], F32, "w1_raw0")]
         load_w1(0, w1_raw[0])
         idx2 = load_list(offs2, "idx2")
         for q in range(4):
-            nc.sync.dma_start(tab2s[32 * q:32 * q + 8, :].bitcast(I32),
-                              tab2_scales[:, 4 * q:4 * q + 4, :].bitcast(I32))
+            nc.gpsimd.dma_start(tab2s[32 * q:32 * q + 8, :].bitcast(I32),
+                                tab2_scales[:, 4 * q:4 * q + 4, :].bitcast(I32))
         tab[0] = load_table(0)
         left = load_list(pos1, "left")
         right = load_list(pos2, "right")
@@ -104,10 +103,11 @@ def tile_list_shelf_neighbour_features_kernel(
         nc.sync.dma_start(fit_sb[:], fit.rearrange("(m p) j -> p m j", p=P))
 
         w4_dealt = kept([P, 4, 4, 2 * P], U8, "w4_dealt")
-        nc.vector.tensor_copy(w4_dealt[:].bitcast(U16),
-                              w4_raw[:].bitcast(U16).rearrange("p a (b m t) -> p (a b) t m", b=2, t=4))
+        nc.vector.tensor_copy(w4_dealt[:].bitcast(U16).rearrange("p g t (c i) -> p g c t i", i=8),
+                              w4_raw[:].bitcast(U16).rearrange("p a (b c i t) -> p (a b) c t i", b=2, i=8, t=4))
         w4s_dealt = kept([P, 4, 4, P], U8, "w4s_dealt")
-        nc.vector.tensor_copy(w4s_dealt[:], w4s_raw[:].rearrange("p a (b m t) -> p (a b) t m", b=2, t=4))
+        nc.vector.tensor_copy(w4s_dealt[:].rearrange("p g t (c i) -> p g c t i", i=16),
+                              w4s_raw[:].rearrange("p a (b c i t) -> p (a b) c t i", b=2, i=16, t=4))
 
         w1_bf, w1_codes, w1_scales = {}, {}, {}
 
@@ -121,7 +121,7 @@ def tile_list_shelf_neighbour_features_kernel(
             w1_scales[b] = kept([P, HALF], U8, f"w1_scales{b}")
             nc.vector.quantize_mx(out=w1_codes[b][:].bitcast(FP8X4), scales=w1_scales[b][:], in_=w1_bf[b][:])
 
-        v_words = {a: kept([P, S], U32, f"v_words{a}") for a in (1, 2)}
+        v_words = {1: kept([P, S], U32, "v_words1")}
         v_scales = [kept([P, S], U8, f"v_scales{w}") for w in range(2)]
 
         def first_stage_pass(acc, a, b, t, h, start, stop):
@@ -139,14 +139,15 @@ def tile_list_shelf_neighbour_features_kernel(
 
         nc.vector.tensor_copy(v_words[1][:], tab[1][:].bitcast(U32).indirect(idx[:]))
         nc.vector.tensor_copy(v_scales[0][:], tabs[:, :T].indirect(idx[:]))
-        nc.vector.tensor_copy(v_words[2][:], tab[2][:].bitcast(U32).indirect(idx[:]))
         nc.vector.tensor_copy(v_scales[1][:], tabs[:, T:].indirect(idx[:]))
+        v_words[2] = keep.tile([P, S], U32, name="v_words2", tag="tabs", align_bytes=64)
+        nc.vector.tensor_copy(v_words[2][:], tab[2][:].bitcast(U32).indirect(idx[:]))
         round_w1(0)
         v2_scales = kept([P, S2], U8, "v2_scales")
         nc.vector.tensor_copy(v2_scales[:], tab2s[:].indirect(idx2[:]))
         quantize_w1(0)
 
-        v_words[0] = keep.tile([P, S], U32, name="v_words0", tag="tabs", align_bytes=64)
+        v_words[0] = keep.tile([P, S], U32, name="v_words0", tag="tab2s", align_bytes=64)
         acc = {}
         for t in range(4):
             for h in range(2):
@@ -189,12 +190,13 @@ def tile_list_shelf_neighbour_features_kernel(
 
         def weave(planes):
             woven = woven_tile(planes.shape[2])
-            nc.scalar.copy(woven[:], planes.rearrange("p t j -> p j t"))
+            nc.scalar.copy(woven[:].rearrange("p (c i) t -> p c t i", i=4), planes.rearrange("p t (c i) -> p c t i", i=4))
             return woven
 
         def weave_abs(planes):
             woven = woven_tile(planes.shape[2])
-            nc.scalar.activation(woven[:], planes.rearrange("p t j -> p j t"), ACT.Abs)
+            nc.scalar.activation(woven[:].rearrange("p (c i) t -> p c t i", i=4),
+                                 planes.rearrange("p t (c i) -> p c t i", i=4), ACT.Abs)
             return woven
 
         def quantize(woven):

@@ -67,8 +67,9 @@ def tile_list_shelf_neighbour_features_kernel(
 
         tab = {1: load_table(1)}
         for r in range(4):
-            nc.gpsimd.dma_start(tabs[r:P:32, :].bitcast(I32).rearrange("q (a c) -> q a c", a=2),
-                                tab_scales[1:3, r:16:4, :].rearrange("a q c -> q a c").bitcast(I32))
+            nc.sync.dma_start(tabs[r:P:32, :].bitcast(I32).rearrange("q (a c) -> q a c", a=2),
+                              tab_scales[1:3, r:16:4, :].rearrange("a q c -> q a c").bitcast(I32))
+        for r in range(4):
             nc.gpsimd.dma_start(tabs[4 + r:P:32, T:].bitcast(I32), tab_scales[0, r:16:4, :].bitcast(I32))
         tab[2] = load_table(2)
         w1_raw = [kept([P, 4, HALF], F32, "w1_raw0")]

@@ -19,7 +19,6 @@ ACT = mybir.ActivationFunctionType
 P = 128
 HALF = 512
 PAIRS = 256
-CLEAR = 5632
 
 
 def tile_list_shelf_neighbour_features_kernel(
@@ -43,10 +42,11 @@ def tile_list_shelf_neighbour_features_kernel(
 
         w4s_raw = kept([P, 2, H], U8, "w4s_raw")
         nc.gpsimd.memset(w4s_raw[:].rearrange("p a c -> p (a c)").bitcast(I32), 0)
-        tabs = keep.tile([P, 2 * T], U8, name="tabs", tag="tabs", align_bytes=64)
-        nc.vector.memset(tabs[:, :CLEAR].bitcast(I32), 0)
-        nc.gpsimd.memset(tabs[:, CLEAR:].bitcast(I32), 0)
-        tab2s = keep.tile([P, T3], U8, name="tab2s", tag="tab2s", align_bytes=64)
+        tabs1 = kept([P, T], U8, "tabs1")
+        nc.gpsimd.memset(tabs1[:].bitcast(I32), 0)
+        tabs20 = keep.tile([P, T], U8, name="tabs20", tag="tabs", align_bytes=64)
+        nc.vector.memset(tabs20[:].bitcast(I32), 0)
+        tab2s = kept([P, T3], U8, "tab2s")
         nc.vector.memset(tab2s[:].bitcast(I32), 0)
 
         idx = load_list(offs, "idx")
@@ -67,17 +67,14 @@ def tile_list_shelf_neighbour_features_kernel(
 
         tab = {1: load_table(1)}
         for r in range(4):
-            nc.sync.dma_start(tabs[r:P:32, :].bitcast(I32).rearrange("q (a c) -> q a c", a=2),
-                              tab_scales[1:3, r:16:4, :].rearrange("a q c -> q a c").bitcast(I32))
+            nc.gpsimd.dma_start(tabs1[r:P:32, :].bitcast(I32), tab_scales[1, r:16:4, :].bitcast(I32))
         for r in range(4):
-            nc.gpsimd.dma_start(tabs[4 + r:P:32, T:].bitcast(I32), tab_scales[0, r:16:4, :].bitcast(I32))
-        tab[2] = load_table(2)
+            nc.sync.dma_start(tabs20[r:P:32, :].bitcast(I32), tab_scales[2, r:16:4, :].bitcast(I32))
         w1_raw = [kept([P, 4, HALF], F32, "w1_raw0")]
         load_w1(0, w1_raw[0])
-        idx2 = load_list(offs2, "idx2")
-        for q in range(4):
-            nc.gpsimd.dma_start(tab2s[32 * q:32 * q + 8, :].bitcast(I32),
-                                tab2_scales[:, 4 * q:4 * q + 4, :].bitcast(I32))
+        for r in range(4):
+            nc.sync.dma_start(tabs20[4 + r:P:32, :].bitcast(I32), tab_scales[0, r:16:4, :].bitcast(I32))
+        tab[2] = load_table(2)
         tab[0] = load_table(0)
         left = load_list(pos1, "left")
         right = load_list(pos2, "right")
@@ -97,6 +94,10 @@ def tile_list_shelf_neighbour_features_kernel(
         load_shelf(0)
         w1_raw.append(big.tile([P, 4, HALF], F32, name="w1_raw1", tag="big", align_bytes=64))
         load_w1(1, w1_raw[1])
+        idx2 = load_list(offs2, "idx2")
+        for q in range(4):
+            nc.sync.dma_start(tab2s[32 * q:32 * q + 8, :].bitcast(I32),
+                              tab2_scales[:, 4 * q:4 * q + 4, :].bitcast(I32))
         tab2 = big.tile([P, 2, T3], I32, name="tab2", tag="big", align_bytes=64)
         nc.sync.dma_start(tab2[:], tab2_words.rearrange("a p t i -> p a (t i)").bitcast(I32))
         load_shelf(1)
@@ -114,8 +115,8 @@ def tile_list_shelf_neighbour_features_kernel(
 
         def round_w1(b):
             w1_bf[b] = work.tile([P, 4 * HALF], BF16, name="w1_bf", tag="woven", bufs=3, align_bytes=64)
-            nc.scalar.copy(w1_bf[b][:].rearrange("p (t m i) -> p m t i", t=4, i=4),
-                           w1_raw[b][:].rearrange("p i (m t) -> p m t i", t=4))
+            nc.scalar.copy(w1_bf[b][:].rearrange("p (t m i) -> p t m i", t=4, i=4),
+                           w1_raw[b][:].rearrange("p i (m t) -> p t m i", t=4))
 
         def quantize_w1(b):
             w1_codes[b] = kept([P, HALF], U32, f"w1_codes{b}")
@@ -139,16 +140,14 @@ def tile_list_shelf_neighbour_features_kernel(
                                 start=start, stop=stop)
 
         nc.vector.tensor_copy(v_words[1][:], tab[1][:].bitcast(U32).indirect(idx[:]))
-        nc.vector.tensor_copy(v_scales[0][:], tabs[:, :T].indirect(idx[:]))
-        nc.vector.tensor_copy(v_scales[1][:], tabs[:, T:].indirect(idx[:]))
+        nc.vector.tensor_copy(v_scales[0][:], tabs1[:].indirect(idx[:]))
+        nc.vector.tensor_copy(v_scales[1][:], tabs20[:].indirect(idx[:]))
         v_words[2] = keep.tile([P, S], U32, name="v_words2", tag="tabs", align_bytes=64)
-        nc.vector.tensor_copy(v_words[2][:], tab[2][:].bitcast(U32).indirect(idx[:]))
         round_w1(0)
-        v2_scales = kept([P, S2], U8, "v2_scales")
-        nc.vector.tensor_copy(v2_scales[:], tab2s[:].indirect(idx2[:]))
         quantize_w1(0)
+        nc.vector.tensor_copy(v_words[2][:], tab[2][:].bitcast(U32).indirect(idx[:]))
 
-        v_words[0] = keep.tile([P, S], U32, name="v_words0", tag="tab2s", align_bytes=64)
+        v_words[0] = kept([P, S], U32, "v_words0")
         acc = {}
         for t in range(4):
             for h in range(2):
@@ -209,6 +208,7 @@ def tile_list_shelf_neighbour_features_kernel(
             return codes, scales
 
         v2_words = kept([P, 2, S2], U32, "v2_words")
+        v2_scales = kept([P, S2], U8, "v2_scales")
         sums = {}
 
         def second_stage(operand, b, halves, start, stop):
@@ -249,6 +249,7 @@ def tile_list_shelf_neighbour_features_kernel(
             else:
                 make_hidden(*ahead[t])
         x1_woven, x2_woven = weave(capped[:]), weave_abs(rights[:])
+        nc.vector.tensor_copy(v2_scales[:], tab2s[:].indirect(idx2[:]))
         for a in range(2):
             nc.vector.tensor_copy(v2_words[:, a, :], tab2[:, a, :].bitcast(U32).indirect(idx2[:]))
 

from contextlib import ExitStack

import concourse.mybir as mybir

K, T, H, S, S2, T3, NP = 1536, 4096, 1024, 1024, 512, 2048, 512
FLOPS = 2 * K * H * S + 2 * 2 * H * S2 * NP

F32 = mybir.dt.float32
BF16 = mybir.dt.bfloat16
I32 = mybir.dt.int32
U32 = mybir.dt.uint32
U16 = mybir.dt.uint16
U8 = mybir.dt.uint8
FP8X4 = mybir.dt.float8_e4m3fn_x4
FP4X4 = mybir.dt.float4_e2m1fn_x4
ALU = mybir.AluOpType
ACT = mybir.ActivationFunctionType

P = 128
HALF = 512
PAIRS = 256


def tile_list_shelf_neighbour_features_kernel(
    tc, tab_words, tab_scales, offs, w1, w4_words, w4_scales, shelf, gain, pos1, pos2, cap,
    tab2_words, tab2_scales, offs2, fit, out,
):
    nc = tc.nc
    with ExitStack() as ctx:
        keep = ctx.enter_context(tc.tile_pool(name="keep", bufs=1))
        big = ctx.enter_context(tc.tile_pool(name="big", bufs=3))
        work = ctx.enter_context(tc.tile_pool(name="work", bufs=2))
        psum = ctx.enter_context(tc.psum_pool(name="psum", bufs=4))

        def load_list(src, name):
            tile = keep.tile([P, src.shape[1]], U16, name=name)
            nc.sync.dma_start(tile[:], src)
            return tile

        def kept(shape, dtype, name):
            return keep.tile(shape, dtype, name=name, align_bytes=64)

        w4s_raw = kept([P, 2, H], U8, "w4s_raw")
        nc.gpsimd.memset(w4s_raw[:].rearrange("p a c -> p (a c)").bitcast(I32), 0)
        tabs1 = kept([P, T], U8, "tabs1")
        nc.gpsimd.memset(tabs1[:].bitcast(I32), 0)
        tabs20 = keep.tile([P, T], U8, name="tabs20", tag="tabs", align_bytes=64)
        nc.vector.memset(tabs20[:].bitcast(I32), 0)
        tab2s = kept([P, T3], U8, "tab2s")
        nc.vector.memset(tab2s[:].bitcast(I32), 0)

        idx = load_list(offs, "idx")
        w4_raw = kept([P, 2, 2 * H], U8, "w4_raw")
        nc.sync.dma_start(w4_raw[:].bitcast(I32), w4_words.rearrange("a p c -> p a c").bitcast(I32))

        for r in range(4):
            nc.sync.dma_start(w4s_raw[r:P:32, :, :].bitcast(I32),
                                w4_scales[:, r:16:4, :].rearrange("a q c -> q a c").bitcast(I32))

        def load_table(a):
            tile = big.tile([P, T], I32, name=f"tab{a}", tag="big", align_bytes=64)
            nc.sync.dma_start(tile[:], tab_words[a].rearrange("p t i -> p (t i)").bitcast(I32))
            return tile

        def load_w1(b, tile):
            nc.sync.dma_start(tile[:], w1[:, b * HALF:(b + 1) * HALF].rearrange("(p i) c -> p i c", i=4))

        tab = {1: load_table(1)}
        for r in range(4):
            nc.gpsimd.dma_start(tabs1[r:P:32, :].bitcast(I32), tab_scales[1, r:16:4, :].bitcast(I32))
        for r in range(4):
            nc.sync.dma_start(tabs20[r:P:32, :].bitcast(I32), tab_scales[2, r:16:4, :].bitcast(I32))
        w1_raw = [kept([P, 4, HALF], F32, "w1_raw0")]
        load_w1(0, w1_raw[0])
        for r in range(4):
            nc.sync.dma_start(tabs20[4 + r:P:32, :].bitcast(I32), tab_scales[0, r:16:4, :].bitcast(I32))
        tab[2] = load_table(2)
        tab[0] = load_table(0)
        left = load_list(pos1, "left")
        right = load_list(pos2, "right")
        gain_sb = kept([P, 2, 4], F32, "gain_sb")
        nc.sync.dma_start(gain_sb[:], gain.rearrange("(b p t) -> p b t", b=2, t=4))
        cap_sb = kept([P, 2, 4], F32, "cap_sb")
        nc.sync.dma_start(cap_sb[:], cap.rearrange("(b p t) -> p b t", b=2, t=4))

        shelf_rows = shelf.rearrange("(b p t) j -> b t p j", b=2, t=4)
        pre = {}

        def load_shelf(b):
            for t in range(4):
                pre[b, t] = kept([P, S], F32, f"pre{b}{t}")
                nc.sync.dma_start(pre[b, t][:], shelf_rows[b, t])

        load_shelf(0)
        w1_raw.append(big.tile([P, 4, HALF], F32, name="w1_raw1", tag="big", align_bytes=64))
        load_w1(1, w1_raw[1])
        idx2 = load_list(offs2, "idx2")
        for q in range(4):
            nc.sync.dma_start(tab2s[32 * q:32 * q + 8, :].bitcast(I32),
                              tab2_scales[:, 4 * q:4 * q + 4, :].bitcast(I32))
        tab2 = big.tile([P, 2, T3], I32, name="tab2", tag="big", align_bytes=64)
        nc.sync.dma_start(tab2[:], tab2_words.rearrange("a p t i -> p a (t i)").bitcast(I32))
        load_shelf(1)
        fit_sb = big.tile([P, 4, NP], F32, name="fit_sb", tag="big", align_bytes=64)
        nc.sync.dma_start(fit_sb[:], fit.rearrange("(m p) j -> p m j", p=P))

        w4_dealt = kept([P, 4, 4, 2 * P], U8, "w4_dealt")
        nc.vector.tensor_copy(w4_dealt[:].bitcast(U16).rearrange("p g t (c i) -> p g c t i", i=8),
                              w4_raw[:].bitcast(U16).rearrange("p a (b c i t) -> p (a b) c t i", b=2, i=8, t=4))
        w4s_dealt = kept([P, 4, 4, P], U8, "w4s_dealt")
        nc.vector.tensor_copy(w4s_dealt[:].rearrange("p g t (c i) -> p g c t i", i=16),
                              w4s_raw[:].rearrange("p a (b c i t) -> p (a b) c t i", b=2, i=16, t=4))

        w1_bf, w1_codes, w1_scales = {}, {}, {}

        def round_w1(b):
            w1_bf[b] = work.tile([P, 4 * HALF], BF16, name="w1_bf", tag="woven", bufs=3, align_bytes=64)
            nc.scalar.copy(w1_bf[b][:].rearrange("p (t m i) -> p t m i", t=4, i=4),
                           w1_raw[b][:].rearrange("p i (m t) -> p t m i", t=4))

        def quantize_w1(b):
            w1_codes[b] = kept([P, HALF], U32, f"w1_codes{b}")
            w1_scales[b] = kept([P, HALF], U8, f"w1_scales{b}")
            nc.vector.quantize_mx(out=w1_codes[b][:].bitcast(FP8X4), scales=w1_scales[b][:], in_=w1_bf[b][:])

        v_words = {1: kept([P, S], U32, "v_words1")}
        v_scales = [kept([P, S], U8, f"v_scales{w}") for w in range(2)]

        def first_stage_pass(acc, a, b, t, h, start, stop):
            cols = slice(h * HALF, (h + 1) * HALF)
            if a == 0:
                ch = slice(t * P, (t + 1) * P)
                lhsT, lhsT_scale = w1_codes[b][:, ch].bitcast(FP8X4), w1_scales[b][:, ch]
                rhs_scale = v_scales[1][4:P, cols]
            else:
                lhsT, lhsT_scale = w4_dealt[:, 2 * (a - 1) + b, t, :].bitcast(FP4X4), w4s_dealt[:, 2 * (a - 1) + b, t, :]
                rhs_scale = v_scales[a - 1][:, cols]
            nc.tensor.matmul_mx(out=acc[:], lhsT=lhsT, lhsT_scale=lhsT_scale,
                                rhs=v_words[a][:, cols].bitcast(FP8X4), rhs_scale=rhs_scale,
                                start=start, stop=stop)

        nc.vector.tensor_copy(v_words[1][:], tab[1][:].bitcast(U32).indirect(idx[:]))
        nc.vector.tensor_copy(v_scales[0][:], tabs1[:].indirect(idx[:]))
        nc.vector.tensor_copy(v_scales[1][:], tabs20[:].indirect(idx[:]))
        v_words[2] = keep.tile([P, S], U32, name="v_words2", tag="tabs", align_bytes=64)
        round_w1(0)
        quantize_w1(0)
        nc.vector.tensor_copy(v_words[2][:], tab[2][:].bitcast(U32).indirect(idx[:]))

        v_words[0] = kept([P, S], U32, "v_words0")
        acc = {}
        for t in range(4):
            for h in range(2):
                acc[0, t, h] = psum.tile([P, HALF], F32, name="acc", tag="early" if t < 2 else "late")
        for a in (1, 2):
            for t in range(4):
                for h in range(2):
                    first_stage_pass(acc[0, t, h], a, 0, t, h, a == 1, False)
        for h in range(2):
            nc.vector.tensor_copy(v_words[0][:, h * HALF:(h + 1) * HALF],
                                  tab[0][:].bitcast(U32).indirect(idx[:, h * 32:(h + 1) * 32]))
            for t in range(4):
                first_stage_pass(acc[0, t, h], 0, 0, t, h, False, True)

        hidden = {}

        def make_hidden(b, t):
            for h in range(2):
                if b == 1:
                    acc[b, t, h] = psum.tile([P, HALF], F32, name="acc", tag="early")
                    for a in (1, 2, 0):
                        first_stage_pass(acc[b, t, h], a, b, t, h, a == 1, a == 0)
                cols = slice(h * HALF, (h + 1) * HALF)
                nc.vector.tensor_tensor(pre[b, t][:, cols], acc[b, t, h][:], pre[b, t][:, cols], ALU.add)
            nc.scalar.activation(pre[b, t][:], pre[b, t][:], ACT.Tanh)
            hidden[b, t] = work.tile([P, S], F32, name="hidden", bufs=5)
            nc.scalar.activation(hidden[b, t][:], pre[b, t][:], ACT.Copy, scale=gain_sb[:, b, t:t + 1])

        def picked_tile(shape, tag):
            return work.tile(shape, F32, name="picked", tag=tag, bufs=1, align_bytes=64)

        def pick(dst, b, t, offsets):
            nc.vector.tensor_copy(dst[:, t, :], hidden[b, t][:].indirect(offsets))

        def cap_plane(dst, src, b, t):
            nc.vector.tensor_scalar(dst[:, t, :], src[:, t, :], cap_sb[:, b, t:t + 1], None, ALU.min)

        def woven_tile(width):
            return work.tile([P, width, 4], BF16, name="woven", tag="woven", bufs=3, align_bytes=64)

        def weave(planes):
            woven = woven_tile(planes.shape[2])
            nc.scalar.copy(woven[:].rearrange("p (c i) t -> p c t i", i=4), planes.rearrange("p t (c i) -> p c t i", i=4))
            return woven

        def weave_abs(planes):
            woven = woven_tile(planes.shape[2])
            nc.scalar.activation(woven[:].rearrange("p (c i) t -> p c t i", i=4),
                                 planes.rearrange("p t (c i) -> p c t i", i=4), ACT.Abs)
            return woven

        def quantize(woven):
            width = woven.shape[1]
            codes = work.tile([P, width], U32, name="codes", bufs=3, align_bytes=64)
            scales = work.tile([P, width], U8, name="scales", bufs=3, align_bytes=64)
            nc.vector.quantize_mx(out=codes[:].bitcast(FP8X4), scales=scales[:],
                                  in_=woven[:].rearrange("p j t -> p (j t)"))
            return codes, scales

        v2_words = kept([P, 2, S2], U32, "v2_words")
        v2_scales = kept([P, S2], U8, "v2_scales")
        sums = {}

        def second_stage(operand, b, halves, start, stop):
            codes, scales = operand
            for n, half in enumerate(halves):
                cols = slice(n * PAIRS, (n + 1) * PAIRS)
                for g in range(2):
                    if start:
                        sums[g, half] = psum.tile([P, 2, PAIRS], F32, name="sums", tag="late")
                    for u in range(2):
                        m = slice((2 * g + u) * P, (2 * g + u + 1) * P)
                        nc.tensor.matmul_mx(out=sums[g, half][:, u, :],
                                            lhsT=v2_words[:, b, m].bitcast(FP8X4), lhsT_scale=v2_scales[4 * b:P, m],
                                            rhs=codes[:, cols].bitcast(FP8X4), rhs_scale=scales[:, cols],
                                            start=start and u == 0, stop=stop and u == 1)

        out_rows = out.rearrange("(m p) j -> p m j", p=P)

        def finish(half):
            cols = slice(half * PAIRS, (half + 1) * PAIRS)
            for g in range(2):
                result = work.tile([P, 2, PAIRS], F32, name="result", bufs=4)
                nc.vector.tensor_tensor(result[:], sums[g, half][:], fit_sb[:, 2 * g:2 * g + 2, cols], ALU.mult)
                nc.sync.dma_start(out_rows[:, 2 * g:2 * g + 2, cols], result[:])

        for t in range(3):
            make_hidden(0, t)
        round_w1(1)
        lefts, rights = picked_tile([P, 4, NP], "picked_a"), picked_tile([P, 4, NP], "picked_b")
        capped = work.tile([P, 4, NP], BF16, name="capped")
        ahead = [(0, 3), None, (1, 0), (1, 1)]
        for t in range(4):
            pick(lefts, 0, t, left[:])
            pick(rights, 0, t, right[:])
            cap_plane(capped, lefts, 0, t)
            if ahead[t] is None:
                quantize_w1(1)
            else:
                make_hidden(*ahead[t])
        x1_woven, x2_woven = weave(capped[:]), weave_abs(rights[:])
        nc.vector.tensor_copy(v2_scales[:], tab2s[:].indirect(idx2[:]))
        for a in range(2):
            nc.vector.tensor_copy(v2_words[:, a, :], tab2[:, a, :].bitcast(U32).indirect(idx2[:]))

        lefts = picked_tile([P, 4, NP], "picked_a")
        capped = work.tile([P, 4, NP], BF16, name="capped")
        for t in range(4):
            pick(lefts, 1, t, left[:])
            if t < 2:
                make_hidden(1, t + 2)
            elif t == 2:
                second_stage(quantize(x1_woven), 0, (0, 1), True, False)
            else:
                second_stage(quantize(x2_woven), 0, (0, 1), False, False)
            cap_plane(capped, lefts, 1, t)
        x1_woven = weave(capped[:])
        rights = picked_tile([P, 2, 4, PAIRS], "picked_a")
        halves = []
        for half in range(2):
            for t in range(4):
                pick(rights[:, half, :, :], 1, t, right[:, half * 16:(half + 1) * 16])
            halves.append(weave_abs(rights[:, half, :, :]))
            if half == 0:
                second_stage(quantize(x1_woven), 1, (0, 1), False, False)
        for half in range(2):
            second_stage(quantize(halves[half]), 1, (half,), False, True)
            finish(half)
